import numpy as np
import ml_dtypes


def mxq(x, axis, fmt="e4m3"):
    dtype, down = {"e4m3": (ml_dtypes.float8_e4m3fn, 7), "e5m2": (ml_dtypes.float8_e5m2, 14)}[fmt]
    v = np.moveaxis(np.asarray(x, np.float32).astype(ml_dtypes.bfloat16).astype(np.float64), axis, -1)
    blocks = v.reshape(v.shape[:-1] + (-1, 32))
    amax = np.abs(blocks).max(-1, keepdims=True)
    byte = np.maximum(np.where(amax > 0, np.frexp(amax)[1] - 1 + 127, 0) - down, 1)
    scale = np.exp2(byte - 127.0)
    codes = (blocks / scale).astype(np.float32).astype(dtype).astype(np.float64)
    return np.moveaxis((codes * scale).reshape(v.shape), -1, axis)


WIDE = False


def mx_kscale(k):
    if not WIDE:
        return np.ones(k)
    levels = np.array([10, -10, 5, -5, 0])
    if k % 512:
        return np.exp2(np.random.permutation(np.resize(levels, k // 32))).repeat(32)
    a = np.empty((k // 512, 16))
    for p in range(k // 512):
        a[p, :8] = np.random.permutation(np.resize(levels, 8))
        for g in range(8):
            far = levels[np.abs(levels - a[p, g]) >= 10]
            a[p, g + 8] = far[np.random.randint(len(far))]
    return np.exp2(a.ravel()).repeat(32)


def f64(x):
    return np.asarray(x).astype(np.float64)


def striped(idx):
    return np.tile(idx.reshape(-1, 16).T, (8, 1)).astype(np.uint16)


def unstriped(offs):
    return offs[:16].T.reshape(-1).astype(np.int64)


E2M1 = np.array([0.0, 0.5, 1.0, 1.5, 2.0, 3.0, 4.0, 6.0, -0.0, -0.5, -1.0, -1.5, -2.0, -3.0, -4.0, -6.0])


def pack_weight(w, fmt):
    k, n = w.shape
    w = f64(np.asarray(w, np.float32).astype(ml_dtypes.bfloat16)).reshape(k // 32, 32, n)
    amax = np.abs(w).max(1)
    if fmt == "e4m3":
        byte = np.frexp(amax)[1] - 1 + 127 - 7
    else:
        mant, ex = np.frexp(amax / 6.0)
        byte = np.where(mant > 0.5, ex, ex - 1) + 127
    byte = np.clip(np.where(amax > 0, byte, 1), 1, 254)
    scaled = (w * np.exp2(127.0 - byte)[:, None, :]).reshape(k, n).astype(np.float32)
    by_word = np.ascontiguousarray(scaled.reshape(k // 512, 128, 4, n).transpose(0, 1, 3, 2))
    if fmt == "e4m3":
        words = by_word.astype(ml_dtypes.float8_e4m3fn).view(np.uint8)
    else:
        c = by_word.astype(ml_dtypes.float4_e2m1fn).view(np.uint8) & 0xF
        words = (c[..., 0::2] | (c[..., 1::2] << 4)).reshape(k // 512, 128, 2 * n)
    return np.ascontiguousarray(words), np.ascontiguousarray(byte.astype(np.uint8).reshape(k // 512, 16, n))


def unpack_weight(words, scales, fmt):
    g, _, n = scales.shape
    words = np.ascontiguousarray(words).reshape(g, 128, n, -1)
    if fmt == "e4m3":
        vals = words.view(ml_dtypes.float8_e4m3fn).astype(np.float64)
    else:
        nib = np.empty((g, 128, n, 4), np.uint8)
        nib[..., 0::2] = words & 0xF
        nib[..., 1::2] = words >> 4
        vals = E2M1[nib]
    vals = vals * np.repeat(np.exp2(scales.astype(np.float64) - 127.0), 8, axis=1)[..., None]
    return vals.transpose(0, 1, 3, 2).reshape(g * 512, n)


def gelu(v):
    return 0.5 * v * (1.0 + np.tanh(np.sqrt(2.0 / np.pi) * (v + 0.044715 * v**3)))


def striped8(idx):
    return np.concatenate([v.reshape(-1, 16).T for v in idx]).astype(np.uint16)


def unstriped8(offs):
    return np.stack([offs[16 * g:16 * g + 16].T.reshape(-1) for g in range(8)]).astype(np.int64)


def heads(h, wgt, idx8):
    r = np.arange(h.shape[0])
    return wgt[r // 4 % 128] * h[r[:, None], idx8[r % 512 // 64]]


def put_heads(h, wgs, idx8, t2):
    r = np.arange(h.shape[0])
    page = np.zeros((h.shape[0], t2))
    page[r[:, None], idx8[r % 512 // 64]] = wgs[r // 4 % 128] * h
    return page


K, T, S, H, P, N, T2 = 1024, 4096, 1024, 1024, 512, 1024, 1024

def setup_inputs():
    n = np.random.standard_normal
    s = mx_kscale(K)[:, None]
    u = mx_kscale(H)[:, None]
    d = {}
    d["tab_words"], d["tab_scales"] = pack_weight(n((K, T)) * s, "e4m3")
    d["offs"] = striped(np.random.permutation(T)[:S])
    d["w1_words"], d["w1_scales"] = pack_weight(n((K, H)) / K**0.5 / s, "e2m1")
    d["lim"] = (0.4 + 0.7 * n((H, S))).astype(np.float32)
    d["gain"] = np.exp(0.4 * n(H)).astype(np.float32)
    d["wgt"] = np.repeat(np.random.uniform(0.5, 2.0, (8, P)), 16, axis=0).astype(np.float32)
    d["offs2"] = striped8(np.stack([np.random.permutation(S)[:P] for _ in range(8)]))
    d["stiff"] = (np.exp(0.3 * n(H)) * u[:, 0]).astype(np.float32)
    d["w2"] = (1.6 * n((H, N)) / H**0.5 / u).astype(np.float32)
    d["wgo"] = np.repeat(np.random.uniform(0.5, 2.0, (8, P)), 16, axis=0).astype(np.float32)
    d["offs3"] = striped8(np.stack([np.random.permutation(T2)[:P] for _ in range(8)]))
    return d

def reference(tab_words, tab_scales, offs, w1_words, w1_scales, lim, gain, wgt, offs2, stiff, w2, wgo, offs3):
    v = unpack_weight(tab_words, tab_scales, "e4m3")[:, unstriped(offs)]
    w1 = unpack_weight(w1_words, w1_scales, "e2m1")
    h = np.minimum(w1.T @ v, f64(lim)) * f64(gain)[:, None]
    x = heads(h, f64(wgt), unstriped8(offs2))
    x = np.tanh(x) * f64(stiff)[:, None]
    z = mxq(f64(w2), 0, "e4m3").T @ mxq(x, 0, "e4m3")
    sq = z * z
    y = sq / (1.0 + sq)
    return put_heads(y, f64(wgo), unstriped8(offs3), T2)

@@ -1,0 +1,232 @@
+from contextlib import ExitStack
+
+import concourse.mybir as mybir
+
+F32 = mybir.dt.float32
+BF16 = mybir.dt.bfloat16
+I32 = mybir.dt.int32
+U32 = mybir.dt.uint32
+U16 = mybir.dt.uint16
+U8 = mybir.dt.uint8
+FP8X4 = mybir.dt.float8_e4m3fn_x4
+FP4X4 = mybir.dt.float4_e2m1fn_x4
+ACT = mybir.ActivationFunctionType
+ALU = mybir.AluOpType
+
+K, T, S, H, M, N, T2 = 1024, 4096, 1024, 1024, 512, 1024, 1024
+P = 128
+PACK = 4
+BANK = 512
+PASSES = 2
+TILES = 8
+PAGES = 4
+TINY = 1e-26
+FLOPS = 2 * K * H * S + 2 * H * N * M
+
+
+def tile_list_spoke_turn_scores_kernel(
+    tc, tab_words, tab_scales, offs, w1_words, w1_scales, lim, gain, wgt, offs2, stiff, w2, wgo, offs3, out
+):
+    nc = tc.nc
+    with ExitStack() as ctx:
+        keep = ctx.enter_context(tc.tile_pool(name="keep", bufs=1))
+        ring = ctx.enter_context(tc.tile_pool(name="ring", bufs=2))
+        psum = ctx.enter_context(tc.psum_pool(name="psum", bufs=4))
+
+        def held(shape, dtype, name, tag=None):
+            return keep.tile(shape, dtype, name=name, tag=tag or name, align_bytes=64)
+
+        list1 = held([P, S // 16], U16, "list1")
+        list2 = held([P, M // 16], U16, "list2")
+        list3 = held([P, M // 16], U16, "list3")
+        w1_raw = held([P, PASSES * 2 * H], U8, "w1_raw")
+        w1_plane_raw = held([P, PASSES * H], U8, "w1_plane_raw")
+        w1_codes = held([P, PASSES * 2 * H], U8, "w1_codes")
+        w1_plane = held([P, PASSES * H], U8, "w1_plane")
+        table = [held([P, T], U32, f"table{a}") for a in range(PASSES)]
+        table_plane = held([P, PASSES * T], U8, "table_plane")
+        v_codes = [[held([P, BANK], U32, f"v_codes{a}{c}") for c in range(2)] for a in range(PASSES)]
+        v_plane = [held([P, S], U8, f"v_plane{a}") for a in range(PASSES)]
+        lim_sb = [held([P, S], F32, f"lim{k}") for k in range(TILES)]
+        w2_raw = [[held([P, PACK, BANK], F32, f"w2_raw{a}{b}") for b in range(2)] for a in range(PASSES)]
+        w2_codes = [[held([P, BANK], U32, f"w2_codes{a}{b}") for b in range(2)] for a in range(PASSES)]
+        w2_plane = [[held([P, BANK], U8, f"w2_plane{a}{b}") for b in range(2)] for a in range(PASSES)]
+        w2_bf = [[held([P, BANK * PACK], BF16, f"w2_bf{a}{b}") for b in range(2)] for a in range(PASSES)]
+        wgt_sb = held([P, M], F32, "wgt_sb")
+        wgo_sb = held([P, M], F32, "wgo_sb")
+        gain_sb = held([P, PASSES, PACK], F32, "gain_sb")
+        stiff_sb = held([P, PASSES, PACK], F32, "stiff_sb")
+        x_rows = [held([P, PACK, M], BF16, f"x_rows{a}") for a in range(PASSES)]
+        x_woven = [held([P, M * PACK], BF16, f"x_woven{a}") for a in range(PASSES)]
+        x_codes = [held([P, M], U32, f"x_codes{a}") for a in range(PASSES)]
+        x_plane = [held([P, M], U8, f"x_plane{a}") for a in range(PASSES)]
+
+        lim_rows = lim.rearrange("(b p i) j -> b i p j", p=P, i=PACK)
+        out_rows = out.rearrange("(b p i) c -> b i p c", p=P, i=PACK)
+        w2_rows = w2.rearrange("(a p i) n -> a p i n", p=P, i=PACK)
+
+        def load_table(a):
+            nc.sync.dma_start(table[a][:].bitcast(I32), tab_words[a].rearrange("p t i -> p (t i)").bitcast(I32))
+
+        def load_w2(a, b):
+            nc.sync.dma_start(w2_raw[a][b][:], w2_rows[a][:, :, b * BANK : (b + 1) * BANK])
+
+        def load_lim(k):
+            nc.sync.dma_start(lim_sb[k][:], lim_rows[k // PACK][k % PACK])
+
+        def load_plane(tile, scales):
+            rows = scales.bitcast(I32).rearrange("a r c -> r a c")
+            for q in range(4):
+                dst = tile[32 * q : 32 * q + 4, :].bitcast(I32).rearrange("r (a c) -> r a c", a=PASSES)
+                nc.sync.dma_start(dst, rows[4 * q : 4 * q + 4])
+
+        nc.vector.memset(table_plane[:].bitcast(I32), 0)
+        nc.vector.memset(w1_plane_raw[:].bitcast(I32), 0)
+        nc.sync.dma_start(list1[:], offs)
+        for a in range(PASSES):
+            nc.sync.dma_start(w1_raw[:, a * 2 * H : (a + 1) * 2 * H].bitcast(I32), w1_words[a].bitcast(I32))
+        nc.sync.dma_start(list2[:], offs2)
+        nc.sync.dma_start(list3[:], offs3)
+        nc.sync.dma_start(gain_sb[:], gain.rearrange("(b p i) -> p b i", p=P, i=PACK))
+        nc.sync.dma_start(stiff_sb[:], stiff.rearrange("(b p i) -> p b i", p=P, i=PACK))
+        load_plane(table_plane, tab_scales)
+        load_table(0)
+        load_plane(w1_plane_raw, w1_scales)
+        load_table(1)
+        load_lim(0)
+        nc.sync.dma_start(wgt_sb[:], wgt)
+        load_lim(1)
+        load_w2(0, 0)
+        load_lim(2)
+        load_lim(3)
+        load_w2(1, 0)
+        load_lim(4)
+        load_lim(5)
+        load_w2(0, 1)
+        load_lim(6)
+        load_lim(7)
+        load_w2(1, 1)
+        nc.sync.dma_start(wgo_sb[:], wgo)
+
+        nc.vector.tensor_copy(
+            w1_codes[:].bitcast(U16).rearrange("p (g t q) -> p g t q", t=PACK, q=P),
+            w1_raw[:].bitcast(U16).rearrange("p (g q t) -> p g t q", t=PACK, q=P),
+        )
+        for a in range(PASSES):
+            nc.vector.tensor_copy(v_plane[a][:], table_plane[:, a * T : (a + 1) * T].indirect(list1[:]))
+
+        def gather_words(a):
+            for c in range(2):
+                nc.vector.tensor_copy(v_codes[a][c][:], table[a][:].indirect(list1[:, 32 * c : 32 * (c + 1)]))
+
+        gather_words(0)
+        nc.vector.tensor_copy(
+            w1_plane[:].rearrange("p (g t q) -> p g t q", t=PACK, q=P),
+            w1_plane_raw[:].rearrange("p (g q t) -> p g t q", t=PACK, q=P),
+        )
+        gather_words(1)
+
+        pages = []
+        for u, tag in enumerate(("table_plane", "table0", "w1_plane_raw", "table1")):
+            pages.append(held([P, T2], F32, f"page{u}", tag))
+            nc.gpsimd.memset(pages[u][:], 0.0)
+
+        def cast_w2(a, b):
+            nc.scalar.copy(
+                w2_bf[a][b][:].rearrange("p (t m j) -> p m t j", t=PACK, j=PACK),
+                w2_raw[a][b][:].rearrange("p j (m t) -> p m t j", t=PACK),
+            )
+
+        def quantise_w2(a, b):
+            nc.vector.quantize_mx(out=w2_codes[a][b][:].bitcast(FP8X4), scales=w2_plane[a][b][:], in_=w2_bf[a][b][:])
+
+        def weave_views(a):
+            return (
+                x_woven[a][:].rearrange("p (c e i) -> p c i e", e=4, i=PACK),
+                x_rows[a][:].rearrange("p i (c e) -> p c i e", e=4),
+            )
+
+        def quantise_x(a):
+            nc.vector.quantize_mx(out=x_codes[a][:].bitcast(FP8X4), scales=x_plane[a][:], in_=x_woven[a][:])
+
+        def first_stage(k):
+            b, i = divmod(k, PACK)
+            h = ring.tile([P, S], F32, name="h")
+            for c in range(2):
+                acc = psum.tile([P, BANK], F32, name="acc1")
+                for a in range(PASSES):
+                    col = a * H + k * P
+                    nc.tensor.matmul_mx(
+                        out=acc[:],
+                        lhsT=w1_codes[:, 2 * col : 2 * (col + P)].bitcast(FP4X4),
+                        lhsT_scale=w1_plane[:, col : col + P],
+                        rhs=v_codes[a][c][:].bitcast(FP8X4),
+                        rhs_scale=v_plane[a][:, c * BANK : (c + 1) * BANK],
+                        start=(a == 0),
+                        stop=(a == PASSES - 1),
+                    )
+                cols = slice(c * BANK, (c + 1) * BANK)
+                nc.vector.tensor_tensor(h[:, cols], acc[:], lim_sb[k][:, cols], ALU.min)
+            picked = ring.tile([P, M], F32, name="picked", bufs=4)
+            nc.vector.tensor_tensor(picked[:], h[:].indirect(list2[:]), wgt_sb[:], ALU.mult)
+            bent = ring.tile([P, M], F32, name="bent")
+            nc.scalar.activation(bent[:], picked[:], ACT.Tanh, scale=gain_sb[:, b, i : i + 1])
+            nc.scalar.activation(x_rows[b][:, i, :], bent[:], ACT.Copy, scale=stiff_sb[:, b, i : i + 1])
+
+        def second_stage(k):
+            b, i = divmod(k, PACK)
+            acc = psum.tile([P, M], F32, name="acc2")
+            for a in range(PASSES):
+                nc.tensor.matmul_mx(
+                    out=acc[:],
+                    lhsT=w2_codes[a][b][:, i * P : (i + 1) * P].bitcast(FP8X4),
+                    lhsT_scale=w2_plane[a][b][:, i * P : (i + 1) * P],
+                    rhs=x_codes[a][:].bitcast(FP8X4),
+                    rhs_scale=x_plane[a][:],
+                    start=(a == 0),
+                    stop=(a == PASSES - 1),
+                )
+            sq = ring.tile([P, M], F32, name="sq")
+            nc.scalar.activation(sq[:], acc[:], ACT.Square)
+            root = ring.tile([P, M], F32, name="root")
+            y = ring.tile([P, M], F32, name="y", bufs=3)
+            page = pages[k % PAGES]
+            if k == 0:
+                nc.scalar.activation(root[:], sq[:], ACT.Abs_reciprocal_sqrt, bias=1.0)
+                nc.scalar.activation(y[:], root[:], ACT.Square)
+                scaled = ring.tile([P, M], F32, name="inv")
+                nc.vector.tensor_tensor(scaled[:], sq[:], wgo_sb[:], ALU.mult)
+                nc.vector.tensor_tensor(page[:].indirect(list3[:]), y[:], scaled[:], ALU.mult)
+            else:
+                nc.scalar.activation(root[:], sq[:], ACT.Abs_reciprocal_sqrt, bias=TINY)
+                inv = ring.tile([P, M], F32, name="inv")
+                nc.scalar.activation(inv[:], root[:], ACT.Square)
+                root2 = ring.tile([P, M], F32, name="root2")
+                nc.scalar.activation(root2[:], inv[:], ACT.Abs_reciprocal_sqrt, bias=1.0)
+                nc.scalar.activation(y[:], root2[:], ACT.Square)
+                nc.vector.tensor_tensor(page[:].indirect(list3[:]), y[:], wgo_sb[:], ALU.mult)
+            nc.sync.dma_start(out_rows[b][i], page[:])
+
+        for k in range(TILES):
+            first_stage(k)
+            if k == 1:
+                cast_w2(0, 0)
+            if k == 3:
+                cast_w2(1, 0)
+                quantise_w2(0, 0)
+            if k == 4:
+                nc.scalar.copy(*weave_views(0))
+            if k == 5:
+                cast_w2(0, 1)
+            if k == 6:
+                cast_w2(1, 1)
+        warm = held([P, 1], F32, "warm")
+        nc.scalar.activation(warm[:], x_rows[1][:, PACK - 1, 0:1], ACT.Abs_reciprocal_sqrt, bias=1.0, scale=0.0)
+        quantise_w2(1, 0)
+        quantise_x(0)
+        nc.vector.tensor_copy(*weave_views(1))
+        quantise_w2(0, 1)
+        quantise_x(1)
+        quantise_w2(1, 1)
+        for k in range(TILES):
+            second_stage(k)

@@ -19,7 +19,7 @@ PACK = 4
 BANK = 512
 PASSES = 2
 TILES = 8
-PAGES = 4
+PAGES = 3
 TINY = 1e-26
 FLOPS = 2 * K * H * S + 2 * H * N * M
 
@@ -49,17 +49,19 @@ def tile_list_spoke_turn_scores_kernel(
         v_plane = [held([P, S], U8, f"v_plane{a}") for a in range(PASSES)]
         lim_sb = [held([P, S], F32, f"lim{k}") for k in range(TILES)]
         w2_raw = [[held([P, PACK, BANK], F32, f"w2_raw{a}{b}") for b in range(2)] for a in range(PASSES)]
-        w2_codes = [[held([P, BANK], U32, f"w2_codes{a}{b}") for b in range(2)] for a in range(PASSES)]
+        w2_codes = {}
         w2_plane = [[held([P, BANK], U8, f"w2_plane{a}{b}") for b in range(2)] for a in range(PASSES)]
-        w2_bf = [[held([P, BANK * PACK], BF16, f"w2_bf{a}{b}") for b in range(2)] for a in range(PASSES)]
+        w2_bf = {}
         wgt_sb = held([P, M], F32, "wgt_sb")
         wgo_sb = held([P, M], F32, "wgo_sb")
         gain_sb = held([P, PASSES, PACK], F32, "gain_sb")
         stiff_sb = held([P, PASSES, PACK], F32, "stiff_sb")
         x_rows = [held([P, PACK, M], BF16, f"x_rows{a}") for a in range(PASSES)]
         x_woven = [held([P, M * PACK], BF16, f"x_woven{a}") for a in range(PASSES)]
-        x_codes = [held([P, M], U32, f"x_codes{a}") for a in range(PASSES)]
+        x_codes = {}
         x_plane = [held([P, M], U8, f"x_plane{a}") for a in range(PASSES)]
+
+        pages = [held([P, T2], F32, f"page{u}") for u in range(PAGES)]
 
         lim_rows = lim.rearrange("(b p i) j -> b i p j", p=P, i=PACK)
         out_rows = out.rearrange("(b p i) c -> b i p c", p=P, i=PACK)
@@ -87,26 +89,28 @@ def tile_list_spoke_turn_scores_kernel(
             nc.sync.dma_start(w1_raw[:, a * 2 * H : (a + 1) * 2 * H].bitcast(I32), w1_words[a].bitcast(I32))
         nc.sync.dma_start(list2[:], offs2)
         nc.sync.dma_start(list3[:], offs3)
-        nc.sync.dma_start(gain_sb[:], gain.rearrange("(b p i) -> p b i", p=P, i=PACK))
-        nc.sync.dma_start(stiff_sb[:], stiff.rearrange("(b p i) -> p b i", p=P, i=PACK))
         load_plane(table_plane, tab_scales)
         load_table(0)
         load_plane(w1_plane_raw, w1_scales)
         load_table(1)
         load_lim(0)
         nc.sync.dma_start(wgt_sb[:], wgt)
+        nc.sync.dma_start(gain_sb[:], gain.rearrange("(b p i) -> p b i", p=P, i=PACK))
+        nc.sync.dma_start(stiff_sb[:], stiff.rearrange("(b p i) -> p b i", p=P, i=PACK))
         load_lim(1)
-        load_w2(0, 0)
         load_lim(2)
+        load_w2(0, 0)
         load_lim(3)
-        load_w2(1, 0)
         load_lim(4)
+        load_w2(1, 0)
         load_lim(5)
-        load_w2(0, 1)
         load_lim(6)
         load_lim(7)
-        load_w2(1, 1)
         nc.sync.dma_start(wgo_sb[:], wgo)
+        load_w2(0, 1)
+        load_w2(1, 1)
+        for page in pages:
+            nc.vector.memset(page[:], 0.0)
 
         nc.vector.tensor_copy(
             w1_codes[:].bitcast(U16).rearrange("p (g t q) -> p g t q", t=PACK, q=P),
@@ -126,19 +130,16 @@ def tile_list_spoke_turn_scores_kernel(
         )
         gather_words(1)
 
-        pages = []
-        for u, tag in enumerate(("table_plane", "table0", "w1_plane_raw", "table1")):
-            pages.append(held([P, T2], F32, f"page{u}", tag))
-            nc.gpsimd.memset(pages[u][:], 0.0)
-
-        def cast_w2(a, b):
-            nc.scalar.copy(
-                w2_bf[a][b][:].rearrange("p (t m j) -> p m t j", t=PACK, j=PACK),
+        def cast_w2(a, b, copy, slot=None):
+            w2_bf[a, b] = held([P, BANK * PACK], BF16, f"w2_bf{a}{b}", slot)
+            copy(
+                w2_bf[a, b][:].rearrange("p (t m j) -> p m t j", t=PACK, j=PACK),
                 w2_raw[a][b][:].rearrange("p j (m t) -> p m t j", t=PACK),
             )
 
-        def quantise_w2(a, b):
-            nc.vector.quantize_mx(out=w2_codes[a][b][:].bitcast(FP8X4), scales=w2_plane[a][b][:], in_=w2_bf[a][b][:])
+        def quantise_w2(a, b, slot=None):
+            w2_codes[a, b] = held([P, BANK], U32, f"w2_codes{a}{b}", slot)
+            nc.vector.quantize_mx(out=w2_codes[a, b][:].bitcast(FP8X4), scales=w2_plane[a][b][:], in_=w2_bf[a, b][:])
 
         def weave_views(a):
             return (
@@ -146,7 +147,8 @@ def tile_list_spoke_turn_scores_kernel(
                 x_rows[a][:].rearrange("p i (c e) -> p c i e", e=4),
             )
 
-        def quantise_x(a):
+        def quantise_x(a, slot=None):
+            x_codes[a] = held([P, M], U32, f"x_codes{a}", slot)
             nc.vector.quantize_mx(out=x_codes[a][:].bitcast(FP8X4), scales=x_plane[a][:], in_=x_woven[a][:])
 
         def first_stage(k):
@@ -179,7 +181,7 @@ def tile_list_spoke_turn_scores_kernel(
             for a in range(PASSES):
                 nc.tensor.matmul_mx(
                     out=acc[:],
-                    lhsT=w2_codes[a][b][:, i * P : (i + 1) * P].bitcast(FP8X4),
+                    lhsT=w2_codes[a, b][:, i * P : (i + 1) * P].bitcast(FP8X4),
                     lhsT_scale=w2_plane[a][b][:, i * P : (i + 1) * P],
                     rhs=x_codes[a][:].bitcast(FP8X4),
                     rhs_scale=x_plane[a][:],
@@ -194,7 +196,7 @@ def tile_list_spoke_turn_scores_kernel(
             if k == 0:
                 nc.scalar.activation(root[:], sq[:], ACT.Abs_reciprocal_sqrt, bias=1.0)
                 nc.scalar.activation(y[:], root[:], ACT.Square)
-                scaled = ring.tile([P, M], F32, name="inv")
+                scaled = held([P, M], F32, "scaled")
                 nc.vector.tensor_tensor(scaled[:], sq[:], wgo_sb[:], ALU.mult)
                 nc.vector.tensor_tensor(page[:].indirect(list3[:]), y[:], scaled[:], ALU.mult)
             else:
@@ -209,24 +211,23 @@ def tile_list_spoke_turn_scores_kernel(
 
         for k in range(TILES):
             first_stage(k)
-            if k == 1:
-                cast_w2(0, 0)
-            if k == 3:
-                cast_w2(1, 0)
-                quantise_w2(0, 0)
+            if k == 2:
+                cast_w2(0, 0, nc.scalar.copy)
             if k == 4:
-                nc.scalar.copy(*weave_views(0))
+                cast_w2(1, 0, nc.scalar.copy)
             if k == 5:
-                cast_w2(0, 1)
-            if k == 6:
-                cast_w2(1, 1)
+                nc.scalar.copy(*weave_views(0))
         warm = held([P, 1], F32, "warm")
         nc.scalar.activation(warm[:], x_rows[1][:, PACK - 1, 0:1], ACT.Abs_reciprocal_sqrt, bias=1.0, scale=0.0)
-        quantise_w2(1, 0)
-        quantise_x(0)
+        quantise_w2(0, 0, "lim6")
+        quantise_w2(1, 0, "lim7")
+        quantise_x(0, "wgt_sb")
         nc.vector.tensor_copy(*weave_views(1))
-        quantise_w2(0, 1)
         quantise_x(1)
-        quantise_w2(1, 1)
+        cast_w2(0, 1, nc.vector.tensor_copy, "x_woven1")
+        quantise_w2(0, 1)
         for k in range(TILES):
             second_stage(k)
+            if k == 0:
+                cast_w2(1, 1, nc.vector.tensor_copy, "scaled")
+                quantise_w2(1, 1)

@@ -44,10 +44,11 @@ def tile_list_spoke_turn_scores_kernel(
         w1_codes = held([P, PASSES * 2 * H], U8, "w1_codes")
         w1_plane = held([P, PASSES * H], U8, "w1_plane")
         table = [held([P, T], U32, f"table{a}") for a in range(PASSES)]
-        table_plane = held([P, PASSES * T], U8, "table_plane")
+        table_rows = held([P, T], U8, "table_rows")
+        v_rows = held([P, S], U8, "v_rows")
         v_codes = [[held([P, BANK], U32, f"v_codes{a}{c}") for c in range(2)] for a in range(PASSES)]
         v_plane = [held([P, S], U8, f"v_plane{a}") for a in range(PASSES)]
-        lim_sb = [held([P, S], F32, f"lim{k}") for k in range(TILES)]
+        lim_sb = [[held([P, BANK], F32, f"lim{k}{c}") for c in range(2)] for k in range(TILES)]
         w2_raw = [[held([P, PACK, BANK], F32, f"w2_raw{a}{b}") for b in range(2)] for a in range(PASSES)]
         w2_codes = {}
         w2_plane = [[held([P, BANK], U8, f"w2_plane{a}{b}") for b in range(2)] for a in range(PASSES)]
@@ -61,38 +62,49 @@ def tile_list_spoke_turn_scores_kernel(
         x_codes = {}
         x_plane = [held([P, M], U8, f"x_plane{a}") for a in range(PASSES)]
 
-        pages = [held([P, T2], F32, f"page{u}") for u in range(PAGES)]
 
         lim_rows = lim.rearrange("(b p i) j -> b i p j", p=P, i=PACK)
         out_rows = out.rearrange("(b p i) c -> b i p c", p=P, i=PACK)
         w2_rows = w2.rearrange("(a p i) n -> a p i n", p=P, i=PACK)
 
-        def load_table(a):
-            nc.sync.dma_start(table[a][:].bitcast(I32), tab_words[a].rearrange("p t i -> p (t i)").bitcast(I32))
+        def load_table(a, parts):
+            words = tab_words[a].rearrange("p t i -> p (t i)").bitcast(I32)
+            for u in range(parts):
+                cols = slice(u * T // parts, (u + 1) * T // parts)
+                nc.sync.dma_start(table[a][:, cols].bitcast(I32), words[:, cols])
 
         def load_w2(a, b):
             nc.sync.dma_start(w2_raw[a][b][:], w2_rows[a][:, :, b * BANK : (b + 1) * BANK])
 
         def load_lim(k):
-            nc.sync.dma_start(lim_sb[k][:], lim_rows[k // PACK][k % PACK])
+            for c in range(2):
+                nc.sync.dma_start(lim_sb[k][c][:], lim_rows[k // PACK][k % PACK][:, c * BANK : (c + 1) * BANK])
 
         def load_plane(tile, scales):
             rows = scales.bitcast(I32).rearrange("a r c -> r a c")
             for q in range(4):
                 dst = tile[32 * q : 32 * q + 4, :].bitcast(I32).rearrange("r (a c) -> r a c", a=PASSES)
-                nc.sync.dma_start(dst, rows[4 * q : 4 * q + 4])
+                nc.gpsimd.dma_start(dst, rows[4 * q : 4 * q + 4])
 
-        nc.vector.memset(table_plane[:].bitcast(I32), 0)
         nc.vector.memset(w1_plane_raw[:].bitcast(I32), 0)
-        nc.sync.dma_start(list1[:], offs)
+        nc.vector.memset(table_rows[0:96, :].bitcast(I32), 0)
         for a in range(PASSES):
-            nc.sync.dma_start(w1_raw[:, a * 2 * H : (a + 1) * 2 * H].bitcast(I32), w1_words[a].bitcast(I32))
-        nc.sync.dma_start(list2[:], offs2)
-        nc.sync.dma_start(list3[:], offs3)
-        load_plane(table_plane, tab_scales)
-        load_table(0)
+            nc.vector.memset(v_plane[a][:].bitcast(I32), 0)
+        nc.sync.dma_start(list1[:], offs)
+        nc.sync.dma_start(table_rows[96:128, :].bitcast(I32), tab_scales.bitcast(I32).rearrange("a r c -> (a r) c"))
+        nc.sync.dma_start(
+            w1_raw[:].bitcast(I32).rearrange("p (a c) -> p a c", a=PASSES),
+            w1_words.bitcast(I32).rearrange("a p c -> p a c"),
+        )
+        load_table(0, 4)
         load_plane(w1_plane_raw, w1_scales)
-        load_table(1)
+        load_table(1, 2)
+        nc.vector.tensor_copy(v_rows[:], table_rows[:].indirect(list1[:]))
+        for a, queue in enumerate((nc.scalar, nc.gpsimd)):
+            for q in range(4):
+                row = 96 + 16 * a + 4 * q
+                queue.dma_start(v_plane[a][32 * q : 32 * q + 4, :].bitcast(I32), v_rows[row : row + 4, :].bitcast(I32))
+        nc.sync.dma_start(list2[:], offs2)
         load_lim(0)
         nc.sync.dma_start(wgt_sb[:], wgt)
         nc.sync.dma_start(gain_sb[:], gain.rearrange("(b p i) -> p b i", p=P, i=PACK))
@@ -106,18 +118,19 @@ def tile_list_spoke_turn_scores_kernel(
         load_lim(5)
         load_lim(6)
         load_lim(7)
+        nc.sync.dma_start(list3[:], offs3)
         nc.sync.dma_start(wgo_sb[:], wgo)
         load_w2(0, 1)
         load_w2(1, 1)
-        for page in pages:
-            nc.vector.memset(page[:], 0.0)
 
         nc.vector.tensor_copy(
             w1_codes[:].bitcast(U16).rearrange("p (g t q) -> p g t q", t=PACK, q=P),
             w1_raw[:].bitcast(U16).rearrange("p (g q t) -> p g t q", t=PACK, q=P),
         )
-        for a in range(PASSES):
-            nc.vector.tensor_copy(v_plane[a][:], table_plane[:, a * T : (a + 1) * T].indirect(list1[:]))
+
+        pages = [held([P, T2], F32, f"page{u}", slot) for u, slot in enumerate((None, "table_rows", "w1_raw"))]
+        for page in pages:
+            nc.vector.memset(page[:], 0.0)
 
         def gather_words(a):
             for c in range(2):
@@ -151,9 +164,8 @@ def tile_list_spoke_turn_scores_kernel(
             x_codes[a] = held([P, M], U32, f"x_codes{a}", slot)
             nc.vector.quantize_mx(out=x_codes[a][:].bitcast(FP8X4), scales=x_plane[a][:], in_=x_woven[a][:])
 
-        def first_stage(k):
-            b, i = divmod(k, PACK)
-            h = ring.tile([P, S], F32, name="h")
+        def limit(k):
+            h = ring.tile([P, S], F32, name="h", bufs=3)
             for c in range(2):
                 acc = psum.tile([P, BANK], F32, name="acc1")
                 for a in range(PASSES):
@@ -168,8 +180,12 @@ def tile_list_spoke_turn_scores_kernel(
                         stop=(a == PASSES - 1),
                     )
                 cols = slice(c * BANK, (c + 1) * BANK)
-                nc.vector.tensor_tensor(h[:, cols], acc[:], lim_sb[k][:, cols], ALU.min)
-            picked = ring.tile([P, M], F32, name="picked", bufs=4)
+                nc.vector.tensor_tensor(h[:, cols], acc[:], lim_sb[k][c][:], ALU.min)
+            return h
+
+        def pick(k, h):
+            b, i = divmod(k, PACK)
+            picked = held([P, M], F32, f"picked{k}", f"lim{k + 1}0" if k + 1 < TILES else None)
             nc.vector.tensor_tensor(picked[:], h[:].indirect(list2[:]), wgt_sb[:], ALU.mult)
             bent = ring.tile([P, M], F32, name="bent")
             nc.scalar.activation(bent[:], picked[:], ACT.Tanh, scale=gain_sb[:, b, i : i + 1])
@@ -209,8 +225,11 @@ def tile_list_spoke_turn_scores_kernel(
                 nc.vector.tensor_tensor(page[:].indirect(list3[:]), y[:], wgo_sb[:], ALU.mult)
             nc.sync.dma_start(out_rows[b][i], page[:])
 
+        limited = [limit(0)]
         for k in range(TILES):
-            first_stage(k)
+            if k + 1 < TILES:
+                limited.append(limit(k + 1))
+            pick(k, limited[k])
             if k == 2:
                 cast_w2(0, 0, nc.scalar.copy)
             if k == 4:
@@ -219,8 +238,8 @@ def tile_list_spoke_turn_scores_kernel(
                 nc.scalar.copy(*weave_views(0))
         warm = held([P, 1], F32, "warm")
         nc.scalar.activation(warm[:], x_rows[1][:, PACK - 1, 0:1], ACT.Abs_reciprocal_sqrt, bias=1.0, scale=0.0)
-        quantise_w2(0, 0, "lim6")
-        quantise_w2(1, 0, "lim7")
+        quantise_w2(0, 0, "lim61")
+        quantise_w2(1, 0, "lim71")
         quantise_x(0, "wgt_sb")
         nc.vector.tensor_copy(*weave_views(1))
         quantise_x(1)

from contextlib import ExitStack

import concourse.mybir as mybir

F32 = mybir.dt.float32
BF16 = mybir.dt.bfloat16
I32 = mybir.dt.int32
U32 = mybir.dt.uint32
U16 = mybir.dt.uint16
U8 = mybir.dt.uint8
FP8X4 = mybir.dt.float8_e4m3fn_x4
FP4X4 = mybir.dt.float4_e2m1fn_x4
ACT = mybir.ActivationFunctionType
ALU = mybir.AluOpType

K, T, S, H, M, N, T2 = 1024, 4096, 1024, 1024, 512, 1024, 1024
P = 128
PACK = 4
BANK = 512
PASSES = 2
TILES = 8
PAGES = 3
TINY = 1e-26
FLOPS = 2 * K * H * S + 2 * H * N * M


def tile_list_spoke_turn_scores_kernel(
    tc, tab_words, tab_scales, offs, w1_words, w1_scales, lim, gain, wgt, offs2, stiff, w2, wgo, offs3, out
):
    nc = tc.nc
    with ExitStack() as ctx:
        keep = ctx.enter_context(tc.tile_pool(name="keep", bufs=1))
        ring = ctx.enter_context(tc.tile_pool(name="ring", bufs=2))
        psum = ctx.enter_context(tc.psum_pool(name="psum", bufs=4))

        def held(shape, dtype, name, tag=None):
            return keep.tile(shape, dtype, name=name, tag=tag or name, align_bytes=64)

        list1 = held([P, S // 16], U16, "list1")
        list2 = held([P, M // 16], U16, "list2")
        list3 = held([P, M // 16], U16, "list3")
        w1_raw = held([P, PASSES * 2 * H], U8, "w1_raw")
        w1_plane_raw = held([P, PASSES * H], U8, "w1_plane_raw")
        w1_codes = held([P, PASSES * 2 * H], U8, "w1_codes")
        w1_plane = held([P, PASSES * H], U8, "w1_plane")
        table = [held([P, T], U32, f"table{a}") for a in range(PASSES)]
        table_rows = held([P, T], U8, "table_rows")
        v_rows = held([P, S], U8, "v_rows")
        v_codes = [[held([P, BANK], U32, f"v_codes{a}{c}") for c in range(2)] for a in range(PASSES)]
        v_plane = [held([P, S], U8, f"v_plane{a}") for a in range(PASSES)]
        lim_sb = [[held([P, BANK], F32, f"lim{k}{c}") for c in range(2)] for k in range(TILES)]
        w2_raw = [[held([P, PACK, BANK], F32, f"w2_raw{a}{b}") for b in range(2)] for a in range(PASSES)]
        w2_codes = {}
        w2_plane = [[held([P, BANK], U8, f"w2_plane{a}{b}") for b in range(2)] for a in range(PASSES)]
        w2_bf = {}
        wgt_sb = held([P, M], F32, "wgt_sb")
        wgo_sb = held([P, M], F32, "wgo_sb")
        gain_sb = held([P, PASSES, PACK], F32, "gain_sb")
        stiff_sb = held([P, PASSES, PACK], F32, "stiff_sb")
        x_rows = [held([P, PACK, M], BF16, f"x_rows{a}") for a in range(PASSES)]
        x_woven = [held([P, M * PACK], BF16, f"x_woven{a}") for a in range(PASSES)]
        x_codes = {}
        x_plane = [held([P, M], U8, f"x_plane{a}") for a in range(PASSES)]


        lim_rows = lim.rearrange("(b p i) j -> b i p j", p=P, i=PACK)
        out_rows = out.rearrange("(b p i) c -> b i p c", p=P, i=PACK)
        w2_rows = w2.rearrange("(a p i) n -> a p i n", p=P, i=PACK)

        def load_table(a, parts):
            words = tab_words[a].rearrange("p t i -> p (t i)").bitcast(I32)
            for u in range(parts):
                cols = slice(u * T // parts, (u + 1) * T // parts)
                nc.sync.dma_start(table[a][:, cols].bitcast(I32), words[:, cols])

        def load_w2(a, b):
            nc.sync.dma_start(w2_raw[a][b][:], w2_rows[a][:, :, b * BANK : (b + 1) * BANK])

        def load_lim(k):
            for c in range(2):
                nc.sync.dma_start(lim_sb[k][c][:], lim_rows[k // PACK][k % PACK][:, c * BANK : (c + 1) * BANK])

        def load_plane(tile, scales):
            rows = scales.bitcast(I32).rearrange("a r c -> r a c")
            for q in range(4):
                dst = tile[32 * q : 32 * q + 4, :].bitcast(I32).rearrange("r (a c) -> r a c", a=PASSES)
                nc.gpsimd.dma_start(dst, rows[4 * q : 4 * q + 4])

        nc.vector.memset(w1_plane_raw[:].bitcast(I32), 0)
        nc.vector.memset(table_rows[0:96, :].bitcast(I32), 0)
        for a in range(PASSES):
            nc.vector.memset(v_plane[a][:].bitcast(I32), 0)
        nc.sync.dma_start(list1[:], offs)
        nc.sync.dma_start(table_rows[96:128, :].bitcast(I32), tab_scales.bitcast(I32).rearrange("a r c -> (a r) c"))
        nc.sync.dma_start(
            w1_raw[:].bitcast(I32).rearrange("p (a c) -> p a c", a=PASSES),
            w1_words.bitcast(I32).rearrange("a p c -> p a c"),
        )
        load_table(0, 4)
        load_plane(w1_plane_raw, w1_scales)
        load_table(1, 2)
        nc.vector.tensor_copy(v_rows[:], table_rows[:].indirect(list1[:]))
        for a, queue in enumerate((nc.scalar, nc.gpsimd)):
            for q in range(4):
                row = 96 + 16 * a + 4 * q
                queue.dma_start(v_plane[a][32 * q : 32 * q + 4, :].bitcast(I32), v_rows[row : row + 4, :].bitcast(I32))
        nc.sync.dma_start(list2[:], offs2)
        load_lim(0)
        nc.sync.dma_start(wgt_sb[:], wgt)
        nc.sync.dma_start(gain_sb[:], gain.rearrange("(b p i) -> p b i", p=P, i=PACK))
        nc.sync.dma_start(stiff_sb[:], stiff.rearrange("(b p i) -> p b i", p=P, i=PACK))
        load_lim(1)
        load_lim(2)
        load_w2(0, 0)
        load_lim(3)
        load_lim(4)
        load_w2(1, 0)
        load_lim(5)
        load_lim(6)
        load_lim(7)
        nc.sync.dma_start(list3[:], offs3)
        nc.sync.dma_start(wgo_sb[:], wgo)
        load_w2(0, 1)
        load_w2(1, 1)

        nc.vector.tensor_copy(
            w1_codes[:].bitcast(U16).rearrange("p (g t q) -> p g t q", t=PACK, q=P),
            w1_raw[:].bitcast(U16).rearrange("p (g q t) -> p g t q", t=PACK, q=P),
        )

        pages = [held([P, T2], F32, f"page{u}", slot) for u, slot in enumerate((None, "table_rows", "w1_raw"))]
        for page in pages:
            nc.vector.memset(page[:], 0.0)

        def gather_words(a):
            for c in range(2):
                nc.vector.tensor_copy(v_codes[a][c][:], table[a][:].indirect(list1[:, 32 * c : 32 * (c + 1)]))

        gather_words(0)
        nc.vector.tensor_copy(
            w1_plane[:].rearrange("p (g t q) -> p g t q", t=PACK, q=P),
            w1_plane_raw[:].rearrange("p (g q t) -> p g t q", t=PACK, q=P),
        )
        gather_words(1)

        def cast_w2(a, b, copy, slot=None):
            w2_bf[a, b] = held([P, BANK * PACK], BF16, f"w2_bf{a}{b}", slot)
            copy(
                w2_bf[a, b][:].rearrange("p (t m j) -> p m t j", t=PACK, j=PACK),
                w2_raw[a][b][:].rearrange("p j (m t) -> p m t j", t=PACK),
            )

        def quantise_w2(a, b, slot=None):
            w2_codes[a, b] = held([P, BANK], U32, f"w2_codes{a}{b}", slot)
            nc.vector.quantize_mx(out=w2_codes[a, b][:].bitcast(FP8X4), scales=w2_plane[a][b][:], in_=w2_bf[a, b][:])

        def weave_views(a):
            return (
                x_woven[a][:].rearrange("p (c e i) -> p c i e", e=4, i=PACK),
                x_rows[a][:].rearrange("p i (c e) -> p c i e", e=4),
            )

        def quantise_x(a, slot=None):
            x_codes[a] = held([P, M], U32, f"x_codes{a}", slot)
            nc.vector.quantize_mx(out=x_codes[a][:].bitcast(FP8X4), scales=x_plane[a][:], in_=x_woven[a][:])

        def limit(k):
            h = ring.tile([P, S], F32, name="h", bufs=3)
            for c in range(2):
                acc = psum.tile([P, BANK], F32, name="acc1")
                for a in range(PASSES):
                    col = a * H + k * P
                    nc.tensor.matmul_mx(
                        out=acc[:],
                        lhsT=w1_codes[:, 2 * col : 2 * (col + P)].bitcast(FP4X4),
                        lhsT_scale=w1_plane[:, col : col + P],
                        rhs=v_codes[a][c][:].bitcast(FP8X4),
                        rhs_scale=v_plane[a][:, c * BANK : (c + 1) * BANK],
                        start=(a == 0),
                        stop=(a == PASSES - 1),
                    )
                cols = slice(c * BANK, (c + 1) * BANK)
                nc.vector.tensor_tensor(h[:, cols], acc[:], lim_sb[k][c][:], ALU.min)
            return h

        def pick(k, h):
            b, i = divmod(k, PACK)
            picked = held([P, M], F32, f"picked{k}", f"lim{k + 1}0" if k + 1 < TILES else None)
            nc.vector.tensor_tensor(picked[:], h[:].indirect(list2[:]), wgt_sb[:], ALU.mult)
            bent = ring.tile([P, M], F32, name="bent")
            nc.scalar.activation(bent[:], picked[:], ACT.Tanh, scale=gain_sb[:, b, i : i + 1])
            nc.scalar.activation(x_rows[b][:, i, :], bent[:], ACT.Copy, scale=stiff_sb[:, b, i : i + 1])

        def second_stage(k):
            b, i = divmod(k, PACK)
            acc = psum.tile([P, M], F32, name="acc2")
            for a in range(PASSES):
                nc.tensor.matmul_mx(
                    out=acc[:],
                    lhsT=w2_codes[a, b][:, i * P : (i + 1) * P].bitcast(FP8X4),
                    lhsT_scale=w2_plane[a][b][:, i * P : (i + 1) * P],
                    rhs=x_codes[a][:].bitcast(FP8X4),
                    rhs_scale=x_plane[a][:],
                    start=(a == 0),
                    stop=(a == PASSES - 1),
                )
            sq = ring.tile([P, M], F32, name="sq")
            nc.scalar.activation(sq[:], acc[:], ACT.Square)
            root = ring.tile([P, M], F32, name="root")
            y = ring.tile([P, M], F32, name="y", bufs=3)
            page = pages[k % PAGES]
            if k == 0:
                nc.scalar.activation(root[:], sq[:], ACT.Abs_reciprocal_sqrt, bias=1.0)
                nc.scalar.activation(y[:], root[:], ACT.Square)
                scaled = held([P, M], F32, "scaled")
                nc.vector.tensor_tensor(scaled[:], sq[:], wgo_sb[:], ALU.mult)
                nc.vector.tensor_tensor(page[:].indirect(list3[:]), y[:], scaled[:], ALU.mult)
            else:
                nc.scalar.activation(root[:], sq[:], ACT.Abs_reciprocal_sqrt, bias=TINY)
                inv = ring.tile([P, M], F32, name="inv")
                nc.scalar.activation(inv[:], root[:], ACT.Square)
                root2 = ring.tile([P, M], F32, name="root2")
                nc.scalar.activation(root2[:], inv[:], ACT.Abs_reciprocal_sqrt, bias=1.0)
                nc.scalar.activation(y[:], root2[:], ACT.Square)
                nc.vector.tensor_tensor(page[:].indirect(list3[:]), y[:], wgo_sb[:], ALU.mult)
            nc.sync.dma_start(out_rows[b][i], page[:])

        limited = [limit(0)]
        for k in range(TILES):
            if k + 1 < TILES:
                limited.append(limit(k + 1))
            pick(k, limited[k])
            if k == 2:
                cast_w2(0, 0, nc.scalar.copy)
            if k == 4:
                cast_w2(1, 0, nc.scalar.copy)
            if k == 5:
                nc.scalar.copy(*weave_views(0))
        warm = held([P, 1], F32, "warm")
        nc.scalar.activation(warm[:], x_rows[1][:, PACK - 1, 0:1], ACT.Abs_reciprocal_sqrt, bias=1.0, scale=0.0)
        quantise_w2(0, 0, "lim61")
        quantise_w2(1, 0, "lim71")
        quantise_x(0, "wgt_sb")
        nc.vector.tensor_copy(*weave_views(1))
        quantise_x(1)
        cast_w2(0, 1, nc.vector.tensor_copy, "x_woven1")
        quantise_w2(0, 1)
        for k in range(TILES):
            second_stage(k)
            if k == 0:
                cast_w2(1, 1, nc.vector.tensor_copy, "scaled")
                quantise_w2(1, 1)
